import numpy as np
import ml_dtypes

BF16 = ml_dtypes.bfloat16


def bf(x):
    return np.asarray(x, np.float32).astype(BF16)


def f32(x):
    return np.asarray(x, np.float32)


def f64(x):
    return np.asarray(x).astype(np.float64)


def striped(idx):
    return np.tile(idx.reshape(-1, 16).T, (8, 1))


S, K, M, N, B, Q = 256, 512, 256, 256, 2, 128


def setup_inputs():
    return {"base": bf(np.random.standard_normal((B, M, S))), "x": bf(np.random.standard_normal((K, N))), "w": bf(np.random.standard_normal((K, M)) / np.sqrt(K)), "b": f32(0.5 * np.random.standard_normal((M, 1))), "offs": striped(np.random.permutation(S))}


def reference(base, x, w, b, offs):
    idx = offs[:16].T.reshape(-1)
    z = f64(base).copy()
    for i in range(B):
        z[i][:, idx[i * Q : (i + 1) * Q]] += f64(w).T @ f64(x)[:, i * Q : (i + 1) * Q]
    return np.tanh(z + f64(b))

@@ -1,0 +1,58 @@
+import concourse.mybir as mybir
+from concourse.masks import make_identity
+
+BF16, F32, U16 = mybir.dt.bfloat16, mybir.dt.float32, mybir.dt.uint16
+TANH = mybir.ActivationFunctionType.Tanh
+
+P = 128
+SEQS, FEATURES, TOKENS = 2, 256, 256
+K, PICKED = 512, 256
+PIECE = PICKED // SEQS
+PIECE_COLS = PIECE // 16
+FEATURE_BLOCKS = FEATURES // P
+K_BLOCKS = K // P
+
+FLOPS = 2 * K * FEATURES * PICKED
+
+
+def tile_scatter_matmul_kernel(tc, base, x, w, b, offs, out):
+    nc = tc.nc
+    with (
+        tc.tile_pool(name="held", bufs=1) as held,
+        tc.psum_pool(name="windows", bufs=1) as windows,
+    ):
+        base_tile = held.tile([P, SEQS, FEATURE_BLOCKS, TOKENS], BF16)
+        w_tile = held.tile([P, K_BLOCKS, FEATURES], BF16)
+        x_tile = held.tile([P, K_BLOCKS, PICKED], BF16)
+        offsets = held.tile([P, PICKED // 16], U16)
+        bias = held.tile([P, FEATURE_BLOCKS], F32)
+        identity = held.tile([P, P], BF16)
+
+        nc.sync.dma_start(base_tile[:], base.rearrange("i (a p) t -> p i a t", p=P))
+        nc.sync.dma_start(w_tile[:], w.rearrange("(p c) m -> p c m", p=P))
+        nc.sync.dma_start(x_tile[:], x.rearrange("(p c) n -> p c n", p=P))
+        nc.sync.dma_start(offsets[:], offs)
+        nc.sync.dma_start(bias[:], b.rearrange("(a p) o -> p (a o)", p=P))
+        make_identity(nc, identity[:])
+
+        blocks = [(i, a) for i in range(SEQS) for a in range(FEATURE_BLOCKS)]
+        window = {}
+        for i, a in blocks:
+            window[i, a] = windows.tile([P, TOKENS], F32, name=f"window_{i}_{a}")
+            nc.tensor.matmul(window[i, a][:], identity[:], base_tile[:, i, a, :], start=True, stop=False)
+
+        for i, a in blocks:
+            piece = offsets[:, i * PIECE_COLS : (i + 1) * PIECE_COLS]
+            for c in range(K_BLOCKS):
+                nc.tensor.matmul(
+                    window[i, a][:].indirect(piece),
+                    w_tile[:, c, a * P : (a + 1) * P],
+                    x_tile[:, c, i * PIECE : (i + 1) * PIECE],
+                    start=False,
+                    stop=c == K_BLOCKS - 1,
+                )
+
+        for i, a in blocks:
+            result = held.tile([P, TOKENS], F32, name=f"result_{i}_{a}")
+            nc.scalar.activation(result[:], window[i, a][:], TANH, bias=bias[:, a : a + 1])
+            nc.sync.dma_start(out[i, a * P : (a + 1) * P, :], result[:])

@@ -12,6 +12,9 @@ PIECE_COLS = PIECE // 16
 FEATURE_BLOCKS = FEATURES // P
 K_BLOCKS = K // P
 
+MATMUL_COLS = 512
+WARM_UPS = 4
+
 FLOPS = 2 * K * FEATURES * PICKED
 
 
@@ -34,6 +37,14 @@ def tile_scatter_matmul_kernel(tc, base, x, w, b, offs, out):
         nc.sync.dma_start(offsets[:], offs)
         nc.sync.dma_start(bias[:], b.rearrange("(a p) o -> p (a o)", p=P))
         make_identity(nc, identity[:])
+
+        zeros = held.tile([P, MATMUL_COLS], BF16)
+        nc.vector.memset(zeros[:], 0.0)
+        first_tanh = held.tile([P, 1], F32)
+        nc.scalar.activation(first_tanh[:], zeros[:, 0:1], TANH)
+        spare_bank = windows.tile([P, MATMUL_COLS], F32)
+        for turn in range(WARM_UPS):
+            nc.tensor.matmul(spare_bank[:], zeros[:, 0:P], zeros[:], start=True, stop=True)
 
         blocks = [(i, a) for i in range(SEQS) for a in range(FEATURE_BLOCKS)]
         window = {}

@@ -31,11 +31,11 @@ def tile_scatter_matmul_kernel(tc, base, x, w, b, offs, out):
         bias = held.tile([P, FEATURE_BLOCKS], F32)
         identity = held.tile([P, P], BF16)
 
-        nc.sync.dma_start(base_tile[:], base.rearrange("i (a p) t -> p i a t", p=P))
+        nc.sync.dma_start(base_tile[:], base.rearrange("i (p a) t -> p i a t", p=P))
         nc.sync.dma_start(w_tile[:], w.rearrange("(p c) m -> p c m", p=P))
         nc.sync.dma_start(x_tile[:], x.rearrange("(p c) n -> p c n", p=P))
         nc.sync.dma_start(offsets[:], offs)
-        nc.sync.dma_start(bias[:], b.rearrange("(a p) o -> p (a o)", p=P))
+        nc.sync.dma_start(bias[:], b.rearrange("(p a) o -> p (a o)", p=P))
         make_identity(nc, identity[:])
 
         zeros = held.tile([P, MATMUL_COLS], BF16)
@@ -57,13 +57,14 @@ def tile_scatter_matmul_kernel(tc, base, x, w, b, offs, out):
             for c in range(K_BLOCKS):
                 nc.tensor.matmul(
                     window[i, a][:].indirect(piece),
-                    w_tile[:, c, a * P : (a + 1) * P],
+                    w_tile[:, c, a::FEATURE_BLOCKS],
                     x_tile[:, c, i * PIECE : (i + 1) * PIECE],
                     start=False,
                     stop=c == K_BLOCKS - 1,
                 )
 
+        out_tile = out.rearrange("i (p a) t -> p i a t", p=P)
         for i, a in blocks:
             result = held.tile([P, TOKENS], F32, name=f"result_{i}_{a}")
             nc.scalar.activation(result[:], window[i, a][:], TANH, bias=bias[:, a : a + 1])
-            nc.sync.dma_start(out[i, a * P : (a + 1) * P, :], result[:])
+            nc.sync.dma_start(out_tile[:, i, a, :], result[:])

@@ -11,9 +11,9 @@ PIECE = PICKED // SEQS
 PIECE_COLS = PIECE // 16
 FEATURE_BLOCKS = FEATURES // P
 K_BLOCKS = K // P
+HALF = K_BLOCKS // 2
 
-MATMUL_COLS = 512
-WARM_UPS = 4
+WARM_UPS = 12
 
 FLOPS = 2 * K * FEATURES * PICKED
 
@@ -32,19 +32,22 @@ def tile_scatter_matmul_kernel(tc, base, x, w, b, offs, out):
         identity = held.tile([P, P], BF16)
 
         nc.sync.dma_start(base_tile[:], base.rearrange("i (p a) t -> p i a t", p=P))
-        nc.sync.dma_start(w_tile[:], w.rearrange("(p c) m -> p c m", p=P))
-        nc.sync.dma_start(x_tile[:], x.rearrange("(p c) n -> p c n", p=P))
         nc.sync.dma_start(offsets[:], offs)
+        w_rows = w.rearrange("(p c) m -> p c m", p=P)
+        x_rows = x.rearrange("(p c) n -> p c n", p=P)
+        for first in range(0, K_BLOCKS, HALF):
+            nc.sync.dma_start(w_tile[:, first : first + HALF, :], w_rows[:, first : first + HALF, :])
+            nc.sync.dma_start(x_tile[:, first : first + HALF, :], x_rows[:, first : first + HALF, :])
         nc.sync.dma_start(bias[:], b.rearrange("(p a) o -> p (a o)", p=P))
         make_identity(nc, identity[:])
 
-        zeros = held.tile([P, MATMUL_COLS], BF16)
+        zeros = held.tile([P, P], BF16)
         nc.vector.memset(zeros[:], 0.0)
         first_tanh = held.tile([P, 1], F32)
         nc.scalar.activation(first_tanh[:], zeros[:, 0:1], TANH)
-        spare_bank = windows.tile([P, MATMUL_COLS], F32)
+        spare_bank = windows.tile([P, P], F32)
         for turn in range(WARM_UPS):
-            nc.tensor.matmul(spare_bank[:], zeros[:, 0:P], zeros[:], start=True, stop=True)
+            nc.tensor.matmul(spare_bank[:], zeros[:], zeros[:], start=True, stop=True)
 
         blocks = [(i, a) for i in range(SEQS) for a in range(FEATURE_BLOCKS)]
         window = {}
@@ -52,16 +55,17 @@ def tile_scatter_matmul_kernel(tc, base, x, w, b, offs, out):
             window[i, a] = windows.tile([P, TOKENS], F32, name=f"window_{i}_{a}")
             nc.tensor.matmul(window[i, a][:], identity[:], base_tile[:, i, a, :], start=True, stop=False)
 
-        for i, a in blocks:
-            piece = offsets[:, i * PIECE_COLS : (i + 1) * PIECE_COLS]
-            for c in range(K_BLOCKS):
-                nc.tensor.matmul(
-                    window[i, a][:].indirect(piece),
-                    w_tile[:, c, a::FEATURE_BLOCKS],
-                    x_tile[:, c, i * PIECE : (i + 1) * PIECE],
-                    start=False,
-                    stop=c == K_BLOCKS - 1,
-                )
+        for first in range(0, K_BLOCKS, HALF):
+            for i, a in blocks:
+                piece = offsets[:, i * PIECE_COLS : (i + 1) * PIECE_COLS]
+                for c in range(first, first + HALF):
+                    nc.tensor.matmul(
+                        window[i, a][:].indirect(piece),
+                        w_tile[:, c, a::FEATURE_BLOCKS],
+                        x_tile[:, c, i * PIECE : (i + 1) * PIECE],
+                        start=False,
+                        stop=c == K_BLOCKS - 1,
+                    )
 
         out_tile = out.rearrange("i (p a) t -> p i a t", p=P)
         for i, a in blocks:

@@ -31,7 +31,9 @@ def tile_scatter_matmul_kernel(tc, base, x, w, b, offs, out):
         bias = held.tile([P, FEATURE_BLOCKS], F32)
         identity = held.tile([P, P], BF16)
 
-        nc.sync.dma_start(base_tile[:], base.rearrange("i (p a) t -> p i a t", p=P))
+        base_rows = base.rearrange("i (p a) t -> p i a t", p=P)
+        for i in range(SEQS):
+            nc.sync.dma_start(base_tile[:, i, :, :], base_rows[:, i, :, :])
         nc.sync.dma_start(offsets[:], offs)
         w_rows = w.rearrange("(p c) m -> p c m", p=P)
         x_rows = x.rearrange("(p c) n -> p c n", p=P)

import concourse.mybir as mybir
from concourse.masks import make_identity

BF16, F32, U16 = mybir.dt.bfloat16, mybir.dt.float32, mybir.dt.uint16
TANH = mybir.ActivationFunctionType.Tanh

P = 128
SEQS, FEATURES, TOKENS = 2, 256, 256
K, PICKED = 512, 256
PIECE = PICKED // SEQS
PIECE_COLS = PIECE // 16
FEATURE_BLOCKS = FEATURES // P
K_BLOCKS = K // P
HALF = K_BLOCKS // 2

WARM_UPS = 12

FLOPS = 2 * K * FEATURES * PICKED


def tile_scatter_matmul_kernel(tc, base, x, w, b, offs, out):
    nc = tc.nc
    with (
        tc.tile_pool(name="held", bufs=1) as held,
        tc.psum_pool(name="windows", bufs=1) as windows,
    ):
        base_tile = held.tile([P, SEQS, FEATURE_BLOCKS, TOKENS], BF16)
        w_tile = held.tile([P, K_BLOCKS, FEATURES], BF16)
        x_tile = held.tile([P, K_BLOCKS, PICKED], BF16)
        offsets = held.tile([P, PICKED // 16], U16)
        bias = held.tile([P, FEATURE_BLOCKS], F32)
        identity = held.tile([P, P], BF16)

        base_rows = base.rearrange("i (p a) t -> p i a t", p=P)
        for i in range(SEQS):
            nc.sync.dma_start(base_tile[:, i, :, :], base_rows[:, i, :, :])
        nc.sync.dma_start(offsets[:], offs)
        w_rows = w.rearrange("(p c) m -> p c m", p=P)
        x_rows = x.rearrange("(p c) n -> p c n", p=P)
        for first in range(0, K_BLOCKS, HALF):
            nc.sync.dma_start(w_tile[:, first : first + HALF, :], w_rows[:, first : first + HALF, :])
            nc.sync.dma_start(x_tile[:, first : first + HALF, :], x_rows[:, first : first + HALF, :])
        nc.sync.dma_start(bias[:], b.rearrange("(p a) o -> p (a o)", p=P))
        make_identity(nc, identity[:])

        zeros = held.tile([P, P], BF16)
        nc.vector.memset(zeros[:], 0.0)
        first_tanh = held.tile([P, 1], F32)
        nc.scalar.activation(first_tanh[:], zeros[:, 0:1], TANH)
        spare_bank = windows.tile([P, P], F32)
        for turn in range(WARM_UPS):
            nc.tensor.matmul(spare_bank[:], zeros[:], zeros[:], start=True, stop=True)

        blocks = [(i, a) for i in range(SEQS) for a in range(FEATURE_BLOCKS)]
        window = {}
        for i, a in blocks:
            window[i, a] = windows.tile([P, TOKENS], F32, name=f"window_{i}_{a}")
            nc.tensor.matmul(window[i, a][:], identity[:], base_tile[:, i, a, :], start=True, stop=False)

        for first in range(0, K_BLOCKS, HALF):
            for i, a in blocks:
                piece = offsets[:, i * PIECE_COLS : (i + 1) * PIECE_COLS]
                for c in range(first, first + HALF):
                    nc.tensor.matmul(
                        window[i, a][:].indirect(piece),
                        w_tile[:, c, a::FEATURE_BLOCKS],
                        x_tile[:, c, i * PIECE : (i + 1) * PIECE],
                        start=False,
                        stop=c == K_BLOCKS - 1,
                    )

        out_tile = out.rearrange("i (p a) t -> p i a t", p=P)
        for i, a in blocks:
            result = held.tile([P, TOKENS], F32, name=f"result_{i}_{a}")
            nc.scalar.activation(result[:], window[i, a][:], TANH, bias=bias[:, a : a + 1])
            nc.sync.dma_start(out_tile[:, i, a, :], result[:])
